import numpy as np
import ml_dtypes

BF16 = ml_dtypes.bfloat16


def bf(x):
    return np.asarray(x, np.float32).astype(BF16)


def f32(x):
    return np.asarray(x, np.float32)


def f64(x):
    return np.asarray(x).astype(np.float64)


def striped(idx):
    return np.concatenate([l.reshape(-1, 16).T for l in idx])


def rows(idx, k):
    return np.tile(np.repeat(idx, 16, axis=0), (k // (16 * 8), 1))


def look(tab, idx):
    return np.take_along_axis(f64(tab), rows(idx, len(tab)), axis=1)


K, S, V, N = 128, 2048, 1536, 1536


def silu(v):
    return v / (1.0 + np.exp(-v))


def setup_inputs():
    return {"tab": f32(np.random.standard_normal((2, K, S))), "y": f32(np.random.standard_normal((K, V))), "offs": striped(np.stack([np.random.permutation(S)[:N] for _ in range(8)]))}


def reference(tab, y, offs):
    idx = np.stack([g.T.reshape(-1) for g in np.split(offs, 8)])
    x = (look(tab[0], idx) * f64(y)) * (silu(look(tab[1], idx)))
    return x

@@ -1,0 +1,38 @@
+import concourse.mybir as mybir
+
+F32, U16 = mybir.dt.float32, mybir.dt.uint16
+P = 128
+PLACES = 2048
+N = 1536
+PIECE = 512
+
+FLOPS = 6 * P * N
+
+
+def tile_lookup_vg_mulsilu_out_kernel(tc, tab, y, offs, out):
+    nc = tc.nc
+    mult = mybir.AluOpType.mult
+    silu = mybir.ActivationFunctionType.Silu
+    with (
+        tc.tile_pool(name="held", bufs=1) as held,
+        tc.tile_pool(name="work", bufs=N // PIECE) as work,
+    ):
+        offsets = held.tile([P, N // 16], U16, name="offsets")
+        values = held.tile([P, PLACES], F32, name="values")
+        stream = held.tile([P, N], F32, name="stream")
+        gates = held.tile([P, PLACES], F32, name="gates")
+        nc.sync.dma_start(offsets[:], offs)
+        nc.sync.dma_start(values[:], tab[0])
+        nc.sync.dma_start(stream[:], y)
+        nc.sync.dma_start(gates[:], tab[1])
+
+        for start in range(0, N, PIECE):
+            piece = slice(start, start + PIECE)
+            places = offsets[:, start // 16 : (start + PIECE) // 16]
+            scaled = work.tile([P, PIECE], F32, name="scaled")
+            nc.vector.tensor_tensor(scaled[:], values[:].indirect(places), stream[:, piece], mult)
+            gate = work.tile([P, PIECE], F32, name="gate")
+            nc.scalar.activation(gate[:], gates[:].indirect(places), silu)
+            result = work.tile([P, PIECE], F32, name="result")
+            nc.vector.tensor_tensor(result[:], scaled[:], gate[:], mult)
+            nc.sync.dma_start(out[:, piece], result[:])

@@ -8,6 +8,8 @@ PIECE = 512
 
 FLOPS = 6 * P * N
 
+WARM_COLUMNS = 8
+
 
 def tile_lookup_vg_mulsilu_out_kernel(tc, tab, y, offs, out):
     nc = tc.nc
@@ -25,6 +27,11 @@ def tile_lookup_vg_mulsilu_out_kernel(tc, tab, y, offs, out):
         nc.sync.dma_start(values[:], tab[0])
         nc.sync.dma_start(stream[:], y)
         nc.sync.dma_start(gates[:], tab[1])
+
+        zeros = held.tile([P, WARM_COLUMNS], F32, name="zeros")
+        warm = held.tile([P, WARM_COLUMNS], F32, name="warm")
+        nc.vector.memset(zeros[:], 0.0)
+        nc.scalar.activation(warm[:], zeros[:], silu)
 
         for start in range(0, N, PIECE):
             piece = slice(start, start + PIECE)

@@ -23,10 +23,13 @@ def tile_lookup_vg_mulsilu_out_kernel(tc, tab, y, offs, out):
         values = held.tile([P, PLACES], F32, name="values")
         stream = held.tile([P, N], F32, name="stream")
         gates = held.tile([P, PLACES], F32, name="gates")
+        head = slice(0, N - PIECE)
+        tail = slice(N - PIECE, N)
         nc.sync.dma_start(offsets[:], offs)
         nc.sync.dma_start(values[:], tab[0])
-        nc.sync.dma_start(stream[:], y)
+        nc.sync.dma_start(stream[:, head], y[:, head])
         nc.sync.dma_start(gates[:], tab[1])
+        nc.sync.dma_start(stream[:, tail], y[:, tail])
 
         zeros = held.tile([P, WARM_COLUMNS], F32, name="zeros")
         warm = held.tile([P, WARM_COLUMNS], F32, name="warm")

import concourse.mybir as mybir

F32, U16 = mybir.dt.float32, mybir.dt.uint16
P = 128
PLACES = 2048
N = 1536
PIECE = 512

FLOPS = 6 * P * N

WARM_COLUMNS = 8


def tile_lookup_vg_mulsilu_out_kernel(tc, tab, y, offs, out):
    nc = tc.nc
    mult = mybir.AluOpType.mult
    silu = mybir.ActivationFunctionType.Silu
    with (
        tc.tile_pool(name="held", bufs=1) as held,
        tc.tile_pool(name="work", bufs=N // PIECE) as work,
    ):
        offsets = held.tile([P, N // 16], U16, name="offsets")
        values = held.tile([P, PLACES], F32, name="values")
        stream = held.tile([P, N], F32, name="stream")
        gates = held.tile([P, PLACES], F32, name="gates")
        head = slice(0, N - PIECE)
        tail = slice(N - PIECE, N)
        nc.sync.dma_start(offsets[:], offs)
        nc.sync.dma_start(values[:], tab[0])
        nc.sync.dma_start(stream[:, head], y[:, head])
        nc.sync.dma_start(gates[:], tab[1])
        nc.sync.dma_start(stream[:, tail], y[:, tail])

        zeros = held.tile([P, WARM_COLUMNS], F32, name="zeros")
        warm = held.tile([P, WARM_COLUMNS], F32, name="warm")
        nc.vector.memset(zeros[:], 0.0)
        nc.scalar.activation(warm[:], zeros[:], silu)

        for start in range(0, N, PIECE):
            piece = slice(start, start + PIECE)
            places = offsets[:, start // 16 : (start + PIECE) // 16]
            scaled = work.tile([P, PIECE], F32, name="scaled")
            nc.vector.tensor_tensor(scaled[:], values[:].indirect(places), stream[:, piece], mult)
            gate = work.tile([P, PIECE], F32, name="gate")
            nc.scalar.activation(gate[:], gates[:].indirect(places), silu)
            result = work.tile([P, PIECE], F32, name="result")
            nc.vector.tensor_tensor(result[:], scaled[:], gate[:], mult)
            nc.sync.dma_start(out[:, piece], result[:])
